import numpy as np
import ml_dtypes


def mxq(x, axis, fmt="e4m3"):
    dtype, down = {"e4m3": (ml_dtypes.float8_e4m3fn, 7), "e5m2": (ml_dtypes.float8_e5m2, 14)}[fmt]
    v = np.moveaxis(np.asarray(x, np.float32).astype(ml_dtypes.bfloat16).astype(np.float64), axis, -1)
    blocks = v.reshape(v.shape[:-1] + (-1, 32))
    amax = np.abs(blocks).max(-1, keepdims=True)
    byte = np.maximum(np.where(amax > 0, np.frexp(amax)[1] - 1 + 127, 0) - down, 1)
    scale = np.exp2(byte - 127.0)
    codes = (blocks / scale).astype(np.float32).astype(dtype).astype(np.float64)
    return np.moveaxis((codes * scale).reshape(v.shape), -1, axis)


WIDE = False


def mx_kscale(k):
    if not WIDE:
        return np.ones(k)
    levels = np.array([10, -10, 5, -5, 0])
    if k % 512:
        return np.exp2(np.random.permutation(np.resize(levels, k // 32))).repeat(32)
    a = np.empty((k // 512, 16))
    for p in range(k // 512):
        a[p, :8] = np.random.permutation(np.resize(levels, 8))
        for g in range(8):
            far = levels[np.abs(levels - a[p, g]) >= 10]
            a[p, g + 8] = far[np.random.randint(len(far))]
    return np.exp2(a.ravel()).repeat(32)


def f64(x):
    return np.asarray(x).astype(np.float64)


def striped(idx):
    return np.tile(np.asarray(idx).reshape(-1, 16).T, (8, 1)).astype(np.uint16)


def unstriped(offs):
    return offs[:16].T.reshape(-1).astype(np.int64)


E2M1 = np.array([0.0, 0.5, 1.0, 1.5, 2.0, 3.0, 4.0, 6.0, -0.0, -0.5, -1.0, -1.5, -2.0, -3.0, -4.0, -6.0])


def pack_weight(w, fmt):
    k, n = w.shape
    w = f64(np.asarray(w, np.float32).astype(ml_dtypes.bfloat16)).reshape(k // 32, 32, n)
    amax = np.abs(w).max(1)
    if fmt == "e4m3":
        byte = np.frexp(amax)[1] - 1 + 127 - 7
    else:
        mant, ex = np.frexp(amax / 6.0)
        byte = np.where(mant > 0.5, ex, ex - 1) + 127
    byte = np.clip(np.where(amax > 0, byte, 1), 1, 254)
    scaled = (w * np.exp2(127.0 - byte)[:, None, :]).reshape(k, n).astype(np.float32)
    by_word = np.ascontiguousarray(scaled.reshape(k // 512, 128, 4, n).transpose(0, 1, 3, 2))
    if fmt == "e4m3":
        words = by_word.astype(ml_dtypes.float8_e4m3fn).view(np.uint8)
    else:
        c = by_word.astype(ml_dtypes.float4_e2m1fn).view(np.uint8) & 0xF
        words = (c[..., 0::2] | (c[..., 1::2] << 4)).reshape(k // 512, 128, 2 * n)
    return np.ascontiguousarray(words), np.ascontiguousarray(byte.astype(np.uint8).reshape(k // 512, 16, n))


def unpack_weight(words, scales, fmt):
    g, _, n = scales.shape
    words = np.ascontiguousarray(words).reshape(g, 128, n, -1)
    if fmt == "e4m3":
        vals = words.view(ml_dtypes.float8_e4m3fn).astype(np.float64)
    else:
        nib = np.empty((g, 128, n, 4), np.uint8)
        nib[..., 0::2] = words & 0xF
        nib[..., 1::2] = words >> 4
        vals = E2M1[nib]
    vals = vals * np.repeat(np.exp2(scales.astype(np.float64) - 127.0), 8, axis=1)[..., None]
    return vals.transpose(0, 1, 3, 2).reshape(g * 512, n)


def sigmoid(v):
    return 1.0 / (1.0 + np.exp(-v))


D, K, R, T, I, Q, G, U = 512, 512, 512, 2048, 512, 128, 64, 1024


def setup_inputs():
    n = np.random.standard_normal
    idx2 = np.random.permutation(U)[:I]
    idx = np.random.permutation(T)[:I]
    fd = mx_kscale(D)
    fk = mx_kscale(K)
    fi = mx_kscale(I)
    keysp = pack_weight(n((D, T)) / fd[:, None], "e2m1")
    tabp = pack_weight(n((K, T)) / fk[:, None], "e2m1")
    return {
        "query": (n((D, Q)) * 0.6 / np.sqrt(D) * fd[:, None]).astype(np.float32),
        "keys_words": keysp[0],
        "keys_scales": keysp[1],
        "sharp": (np.random.uniform(1.0, 3.0, (Q, 1))).astype(np.float32),
        "tab_words": tabp[0],
        "tab_scales": tabp[1],
        "w1": (n((K, R)) * 1 / np.sqrt(K) * fk[:, None]).astype(np.float32),
        "gtab": (n((R, U))).astype(np.float32),
        "os": (np.random.uniform(4.0, 16.0, (1, I)) * fi).astype(np.float32),
        "vs": (np.random.uniform(0.5, 2.0, (1, I)) / fi).astype(np.float32),
        "offs2": striped(idx2),
        "offs": striped(idx),
    }


def reference(query, keys_words, keys_scales, sharp, tab_words, tab_scales, w1, gtab, os, vs, offs2, offs):
    idx2 = unstriped(offs2)
    idx = unstriped(offs)
    keysu = unpack_weight(keys_words, keys_scales, "e2m1")
    tabu = unpack_weight(tab_words, tab_scales, "e2m1")
    queryq = mxq(f64(query), 0, "e4m3")
    keysidxg = keysu[:, idx]
    a = queryq.T @ keysidxg
    p = np.exp(a)
    s = p.reshape(Q, G, I // G).sum(axis=2)
    ms = a.reshape(Q, G, I // G).mean(axis=2) * f64(sharp)
    pg = np.exp(ms - np.max(ms, axis=1, keepdims=True))
    z = np.sum(pg, axis=1, keepdims=True)
    sh = pg / z / s
    rr = np.repeat(sh, I // G, axis=1)
    w = p * rr
    w1q = mxq(f64(w1), 0, "e4m3")
    tabidxg = tabu[:, idx]
    zh = w1q.T @ tabidxg
    hg = sigmoid(f64(gtab)[:, idx2])
    hv = zh * hg
    wo1 = w * f64(os)
    wt1 = wo1.T
    hw = hv * f64(vs)
    ht1 = hw.T
    wt1q = mxq(wt1, 0, "e4m3")
    ht1q = mxq(ht1, 0, "e4m3")
    o = wt1q.T @ ht1q
    return o

@@ -1,0 +1,172 @@
+from contextlib import ExitStack
+
+import concourse.mybir as mybir
+from concourse.masks import make_identity
+
+D, K, R, T, I, Q, G, U = 512, 512, 512, 2048, 512, 128, 64, 1024
+FLOPS = 2 * (D * Q * I + K * R * I + I * Q * R)
+
+F32 = mybir.dt.float32
+BF16 = mybir.dt.bfloat16
+I32 = mybir.dt.int32
+U32 = mybir.dt.uint32
+U16 = mybir.dt.uint16
+U8 = mybir.dt.uint8
+FP8X4 = mybir.dt.float8_e4m3fn_x4
+FP4X4 = mybir.dt.float4_e2m1fn_x4
+ALU = mybir.AluOpType
+ACT = mybir.ActivationFunctionType
+AX = mybir.AxisListType
+
+P = 128
+PACK = 4
+GROUP = I // G
+HALF = R // 2
+
+
+def tile_attend_lrgated_bygroup_kernel(tc, query, keys_words, keys_scales, sharp, tab_words, tab_scales, w1, gtab, w_factor, v_factor, offs2, offs, out):
+    nc = tc.nc
+    with ExitStack() as ctx:
+        lists = ctx.enter_context(tc.tile_pool(name="lists", bufs=1))
+        sb = ctx.enter_context(tc.tile_pool(name="sb", bufs=1))
+        ring = ctx.enter_context(tc.tile_pool(name="ring", bufs=2))
+        psum = ctx.enter_context(tc.psum_pool(name="psum", bufs=2))
+        zpsum = ctx.enter_context(tc.psum_pool(name="zpsum", bufs=1))
+
+        slots = lists.tile([P, I // 16], U16, name="slots")
+        gates = lists.tile([P, I // 16], U16, name="gates")
+        key_words = sb.tile([P, T], U16, name="key_words")
+        tab_wordt = sb.tile([P, T], U16, name="tab_wordt")
+        key_bytes = sb.tile([P, T], U8, name="key_bytes")
+        tab_bytes = sb.tile([P, T], U8, name="tab_bytes")
+        q_raw = sb.tile([P, PACK, Q], F32, name="q_raw")
+        w_raw = [sb.tile([P, PACK, HALF], F32, name=f"w_raw{h}") for h in range(2)]
+        g_raw = [sb.tile([P, U], F32, name=f"g_raw{j}") for j in range(4)]
+        rows = sb.tile([P, P], F32, name="rows")
+        ident = sb.tile([P, P], F32, name="ident")
+        warm = sb.tile([P, 1], F32, name="warm")
+        warm2 = sb.tile([P, 1], F32, name="warm2")
+
+        sharp_col = sb.tile([P, 1], F32, name="sharp_col")
+        nc.gpsimd.memset(key_bytes[:].bitcast(I32), 0)
+        nc.vector.memset(warm[:], 0.0)
+        nc.vector.memset(tab_bytes[:].bitcast(I32), 0)
+        nc.vector.memset(rows[:], 0.0)
+        nc.scalar.activation(out=warm2[:], in_=warm[:], func=ACT.Exp)
+        make_identity(nc, ident[:])
+
+        def load_scales(tile, src):
+            for quad in range(4):
+                nc.sync.dma_start(out=tile[32 * quad : 32 * quad + 4, :].bitcast(I32), in_=src[0, 4 * quad : 4 * quad + 4, :].bitcast(I32))
+
+        w_view = w1.rearrange("(p t) r -> p t r", t=PACK)
+        nc.sync.dma_start(slots[:], offs)
+        nc.sync.dma_start(out=key_words[:].bitcast(I32), in_=keys_words[0].bitcast(I32))
+        load_scales(key_bytes, keys_scales)
+        nc.sync.dma_start(out=q_raw[:], in_=query.rearrange("(p t) q -> p t q", t=PACK))
+        nc.sync.dma_start(out=w_raw[0][:], in_=w_view[:, :, 0:HALF])
+        nc.sync.dma_start(out=sharp_col[:], in_=sharp)
+        nc.sync.dma_start(out=w_raw[1][:], in_=w_view[:, :, HALF:R])
+        nc.sync.dma_start(out=tab_wordt[:].bitcast(I32), in_=tab_words[0].bitcast(I32))
+        load_scales(tab_bytes, tab_scales)
+        nc.sync.dma_start(out=g_raw[0][:], in_=gtab[0:P, :])
+        nc.sync.dma_start(gates[:], offs2)
+        nc.sync.dma_start(out=rows[4:8, :].rearrange("t (b j) -> t b j", j=GROUP), in_=w_factor.rearrange("o (b t j) -> (o t) b j", t=PACK, j=GROUP))
+        nc.sync.dma_start(out=rows[0:4, :].rearrange("t (b j) -> t b j", j=GROUP), in_=v_factor.rearrange("o (b t j) -> (o t) b j", t=PACK, j=GROUP))
+        for j in range(1, 4):
+            nc.sync.dma_start(out=g_raw[j][:], in_=gtab[P * j : P * (j + 1), :])
+
+        cols_ps = psum.tile([P, PACK, P], F32, name="cols_ps", tag="turn")
+        nc.tensor.transpose(cols_ps[:, 0, :], rows[:], ident[:])
+        cols = sb.tile([P, 8], F32, name="cols")
+        neg_sharp = sb.tile([P, 1], F32, name="neg_sharp")
+
+        def weave(engine_copy, dst, src):
+            engine_copy(out=dst.rearrange("p (c i) t -> p c t i", i=4), in_=src.rearrange("p t (c i) -> p c t i", i=4))
+
+        def quantise(name, src, width):
+            codes = sb.tile([P, width], U32, name=name + "_codes", align_bytes=64)
+            scales = sb.tile([P, width], U8, name=name + "_scales", align_bytes=64)
+            nc.vector.quantize_mx(out=codes[:].bitcast(FP8X4), scales=scales[:], in_=src.rearrange("p c t -> p (c t)"))
+            return codes, scales
+
+        kw = sb.tile([P, I], U16, name="kw", align_bytes=64)
+        ks = sb.tile([P, I], U8, name="ks", align_bytes=64)
+        tw = sb.tile([P, I], U16, name="tw", align_bytes=64)
+        ts = sb.tile([P, I], U8, name="ts", align_bytes=64)
+        nc.vector.tensor_copy(out=kw[:], in_=key_words[:].indirect(slots[:]))
+        nc.vector.tensor_copy(out=ks[:], in_=key_bytes[:].indirect(slots[:]))
+        nc.vector.tensor_scalar(out=neg_sharp[:], in0=sharp_col[:], scalar1=-1.0 / GROUP, scalar2=None, op0=ALU.mult)
+
+        w_bf = [sb.tile([P, HALF, PACK], BF16, name=f"w_bf{h}", align_bytes=64) for h in range(2)]
+        q_bf = sb.tile([P, Q, PACK], BF16, name="q_bf", align_bytes=64)
+        weave(nc.scalar.copy, q_bf[:], q_raw[:])
+        weave(nc.scalar.copy, w_bf[0][:], w_raw[0][:])
+        q_codes, q_scales = quantise("q", q_bf[:], Q)
+        score = psum.tile([P, I], F32, name="score", tag="acc")
+        nc.tensor.matmul_mx(out=score[:], lhsT=q_codes[:].bitcast(FP8X4), lhsT_scale=q_scales[:], rhs=kw[:].bitcast(FP4X4), rhs_scale=ks[:], start=True, stop=True)
+        w_q = [quantise("w0", w_bf[0][:], HALF)]
+
+        p = sb.tile([P, I], F32, name="p")
+        asum = sb.tile([P, G], F32, name="asum")
+        nms = sb.tile([P, G], F32, name="nms")
+        nmin = sb.tile([P, 1], F32, name="nmin")
+        pg = sb.tile([P, G], F32, name="pg")
+        z = sb.tile([P, 1], F32, name="z")
+        s = sb.tile([P, G], F32, name="s")
+        rs = sb.tile([P, G], F32, name="rs")
+        rz = sb.tile([P, 1], F32, name="rz")
+        sh = sb.tile([P, G], F32, name="sh")
+        nc.vector.tensor_reduce(out=asum[:], in_=score[:].rearrange("q (g j) -> q g j", j=GROUP), axis=AX.X, op=ALU.add)
+        weave(nc.scalar.copy, w_bf[1][:], w_raw[1][:])
+        nc.scalar.activation(out=p[:], in_=score[:], func=ACT.Exp)
+        nc.vector.tensor_scalar(out=nms[:], in0=asum[:], scalar1=neg_sharp[:], scalar2=None, op0=ALU.mult, op1=ALU.min, accum_out=nmin[:])
+        nc.scalar.activation(out=pg[:], in_=nms[:], func=ACT.Exp, scale=-1.0, bias=nmin[:], accum_out=z[:])
+        nc.vector.tensor_copy(out=tw[:], in_=tab_wordt[:].indirect(slots[:]))
+        nc.vector.tensor_reduce(out=s[:], in_=p[:].rearrange("q (g j) -> q g j", j=GROUP), axis=AX.X, op=ALU.add)
+        nc.vector.tensor_copy(out=ts[:], in_=tab_bytes[:].indirect(slots[:]))
+        nc.vector.reciprocal(out=rs[:], in_=s[:])
+        nc.vector.reciprocal(out=rz[:], in_=z[:])
+        w_q.append(quantise("w1", w_bf[1][:], HALF))
+        nc.vector.scalar_tensor_tensor(out=sh[:], in0=pg[:], scalar=rz[:], in1=rs[:], op0=ALU.mult, op1=ALU.mult)
+
+        nc.vector.tensor_copy(out=cols[:], in_=cols_ps[:, 0, 0:8])
+        zh = []
+        for j in range(4):
+            bank = zpsum.tile([P, I], F32, name=f"zh{j}")
+            codes, scales = w_q[j // 2]
+            cs = slice(P * (j % 2), P * (j % 2 + 1))
+            nc.tensor.matmul_mx(out=bank[:], lhsT=codes[:, cs].bitcast(FP8X4), lhsT_scale=scales[:, cs], rhs=tw[:].bitcast(FP4X4), rhs_scale=ts[:], start=True, stop=True)
+            zh.append(bank)
+
+        def dealt(ap):
+            return ap.rearrange("p (b t j) -> p t b j", t=PACK, j=GROUP)
+
+        def turn_scale_quantise(name, src, factor):
+            turned = psum.tile([P, PACK, P], F32, name=name + "_turned", tag="turn")
+            for t in range(PACK):
+                nc.tensor.transpose(turned[:, t, :], src[:, t, :], ident[:])
+            woven = ring.tile([P, P, PACK], BF16, name=name + "_woven", tag="woven", align_bytes=64)
+            nc.vector.tensor_tensor(out=woven[:], in0=turned[:].rearrange("p t c -> p c t"), in1=factor.unsqueeze(1).to_broadcast([P, P, PACK]), op=ALU.mult)
+            return quantise(name, woven[:], P)
+
+        w = ring.tile([P, PACK, P], F32, name="w", tag="dealt")
+        nc.vector.tensor_tensor(
+            out=w[:].rearrange("p t (b j) -> p t b j", j=GROUP), in0=dealt(p[:]),
+            in1=sh[:].rearrange("p (b t) -> p t b", t=PACK).unsqueeze(3).to_broadcast([P, PACK, P // GROUP, GROUP]), op=ALU.mult)
+        wt_codes, wt_scales = turn_scale_quantise("wt", w, cols[:, 4:8])
+
+        for j in range(4):
+            hg = ring.tile([P, I], F32, name=f"hg{j}", tag="hg", bufs=4)
+            nc.scalar.activation(out=hg[:], in_=g_raw[j][:].indirect(gates[:]), func=ACT.Sigmoid)
+            hv = ring.tile([P, PACK, P], F32, name=f"hv{j}", tag="dealt")
+            nc.vector.tensor_tensor(out=hv[:].rearrange("p t (b j) -> p t b j", j=GROUP), in0=dealt(zh[j][:]), in1=dealt(hg[:]), op=ALU.mult)
+            h_codes, h_scales = turn_scale_quantise(f"ht{j}", hv, cols[:, 0:4])
+            if j in (0, 3):
+                acc = psum.tile([P, I], F32, name=f"acc{j}", tag="acc")
+            nc.tensor.matmul_mx(out=acc[:, P * j : P * (j + 1)], lhsT=wt_codes[:].bitcast(FP8X4), lhsT_scale=wt_scales[:], rhs=h_codes[:].bitcast(FP8X4), rhs_scale=h_scales[:], start=True, stop=True)
+            if j >= 2:
+                rs_ = slice(0, 3 * P) if j == 2 else slice(3 * P, R)
+                res = sb.tile([P, R], F32, name=f"res{j}")
+                nc.scalar.copy(out=res[:, rs_], in_=acc[:, rs_])
+                nc.sync.dma_start(out=out[:, rs_], in_=res[:, rs_])

@@ -22,6 +22,7 @@ P = 128
 PACK = 4
 GROUP = I // G
 HALF = R // 2
+CHUNKS = R // P
 
 
 def tile_attend_lrgated_bygroup_kernel(tc, query, keys_words, keys_scales, sharp, tab_words, tab_scales, w1, gtab, w_factor, v_factor, offs2, offs, out):
@@ -29,31 +30,32 @@ def tile_attend_lrgated_bygroup_kernel(tc, query, keys_words, keys_scales, sharp
     with ExitStack() as ctx:
         lists = ctx.enter_context(tc.tile_pool(name="lists", bufs=1))
         sb = ctx.enter_context(tc.tile_pool(name="sb", bufs=1))
-        ring = ctx.enter_context(tc.tile_pool(name="ring", bufs=2))
-        psum = ctx.enter_context(tc.psum_pool(name="psum", bufs=2))
-        zpsum = ctx.enter_context(tc.psum_pool(name="zpsum", bufs=1))
+        psum = ctx.enter_context(tc.psum_pool(name="psum", bufs=1))
 
         slots = lists.tile([P, I // 16], U16, name="slots")
         gates = lists.tile([P, I // 16], U16, name="gates")
-        key_words = sb.tile([P, T], U16, name="key_words")
-        tab_wordt = sb.tile([P, T], U16, name="tab_wordt")
+        key_pool = sb.tile([P, T], U16, name="key_pool")
+        tab_pool = sb.tile([P, T], U16, name="tab_pool")
         key_bytes = sb.tile([P, T], U8, name="key_bytes")
         tab_bytes = sb.tile([P, T], U8, name="tab_bytes")
         q_raw = sb.tile([P, PACK, Q], F32, name="q_raw")
         w_raw = [sb.tile([P, PACK, HALF], F32, name=f"w_raw{h}") for h in range(2)]
-        g_raw = [sb.tile([P, U], F32, name=f"g_raw{j}") for j in range(4)]
-        rows = sb.tile([P, P], F32, name="rows")
+        g_raw = [sb.tile([P, U], F32, name=f"g_raw{j}", align_bytes=64) for j in range(CHUNKS)]
         ident = sb.tile([P, P], F32, name="ident")
         warm = sb.tile([P, 1], F32, name="warm")
         warm2 = sb.tile([P, 1], F32, name="warm2")
-
         sharp_col = sb.tile([P, 1], F32, name="sharp_col")
+        wf_col = sb.tile([P, PACK], F32, name="wf_col")
+        vf_col = sb.tile([P, PACK], F32, name="vf_col")
+
         nc.gpsimd.memset(key_bytes[:].bitcast(I32), 0)
         nc.vector.memset(warm[:], 0.0)
         nc.vector.memset(tab_bytes[:].bitcast(I32), 0)
-        nc.vector.memset(rows[:], 0.0)
         nc.scalar.activation(out=warm2[:], in_=warm[:], func=ACT.Exp)
+        nc.gpsimd.dma_start(out=sharp_col[:], in_=sharp)
+        nc.gpsimd.dma_start(out=vf_col[:], in_=v_factor.rearrange("o (n m) -> (o n) m", m=PACK))
         make_identity(nc, ident[:])
+        nc.gpsimd.dma_start(out=wf_col[:], in_=w_factor.rearrange("o (n m) -> (o n) m", m=PACK))
 
         def load_scales(tile, src):
             for quad in range(4):
@@ -61,53 +63,55 @@ def tile_attend_lrgated_bygroup_kernel(tc, query, keys_words, keys_scales, sharp
 
         w_view = w1.rearrange("(p t) r -> p t r", t=PACK)
         nc.sync.dma_start(slots[:], offs)
-        nc.sync.dma_start(out=key_words[:].bitcast(I32), in_=keys_words[0].bitcast(I32))
+        nc.sync.dma_start(out=key_pool[:].bitcast(I32), in_=keys_words[0].bitcast(I32))
         load_scales(key_bytes, keys_scales)
         nc.sync.dma_start(out=q_raw[:], in_=query.rearrange("(p t) q -> p t q", t=PACK))
+        nc.sync.dma_start(out=tab_pool[:].bitcast(I32), in_=tab_words[0].bitcast(I32))
         nc.sync.dma_start(out=w_raw[0][:], in_=w_view[:, :, 0:HALF])
-        nc.sync.dma_start(out=sharp_col[:], in_=sharp)
-        nc.sync.dma_start(out=w_raw[1][:], in_=w_view[:, :, HALF:R])
-        nc.sync.dma_start(out=tab_wordt[:].bitcast(I32), in_=tab_words[0].bitcast(I32))
         load_scales(tab_bytes, tab_scales)
-        nc.sync.dma_start(out=g_raw[0][:], in_=gtab[0:P, :])
         nc.sync.dma_start(gates[:], offs2)
-        nc.sync.dma_start(out=rows[4:8, :].rearrange("t (b j) -> t b j", j=GROUP), in_=w_factor.rearrange("o (b t j) -> (o t) b j", t=PACK, j=GROUP))
-        nc.sync.dma_start(out=rows[0:4, :].rearrange("t (b j) -> t b j", j=GROUP), in_=v_factor.rearrange("o (b t j) -> (o t) b j", t=PACK, j=GROUP))
-        for j in range(1, 4):
+        nc.sync.dma_start(out=g_raw[0][:], in_=gtab[0:P, :])
+        nc.sync.dma_start(out=w_raw[1][:], in_=w_view[:, :, HALF:R])
+        for j in range(1, CHUNKS):
             nc.sync.dma_start(out=g_raw[j][:], in_=gtab[P * j : P * (j + 1), :])
 
-        cols_ps = psum.tile([P, PACK, P], F32, name="cols_ps", tag="turn")
-        nc.tensor.transpose(cols_ps[:, 0, :], rows[:], ident[:])
-        cols = sb.tile([P, 8], F32, name="cols")
-        neg_sharp = sb.tile([P, 1], F32, name="neg_sharp")
-
-        def weave(engine_copy, dst, src):
-            engine_copy(out=dst.rearrange("p (c i) t -> p c t i", i=4), in_=src.rearrange("p t (c i) -> p c t i", i=4))
+        def spread(name, col, tag):
+            bank = psum.tile([P, PACK, P], F32, name=name, tag=tag)
+            for m in range(PACK):
+                nc.tensor.transpose(bank[:, m, :], col[:, m : m + 1].to_broadcast([P, P]), ident[:])
+            return bank[:].rearrange("p m n -> p n m")
 
         def quantise(name, src, width):
             codes = sb.tile([P, width], U32, name=name + "_codes", align_bytes=64)
             scales = sb.tile([P, width], U8, name=name + "_scales", align_bytes=64)
-            nc.vector.quantize_mx(out=codes[:].bitcast(FP8X4), scales=scales[:], in_=src.rearrange("p c t -> p (c t)"))
+            nc.vector.quantize_mx(out=codes[:].bitcast(FP8X4), scales=scales[:], in_=src)
             return codes, scales
+
 
         kw = sb.tile([P, I], U16, name="kw", align_bytes=64)
         ks = sb.tile([P, I], U8, name="ks", align_bytes=64)
         tw = sb.tile([P, I], U16, name="tw", align_bytes=64)
         ts = sb.tile([P, I], U8, name="ts", align_bytes=64)
-        nc.vector.tensor_copy(out=kw[:], in_=key_words[:].indirect(slots[:]))
+        neg_sharp = sb.tile([P, 1], F32, name="neg_sharp")
+        nc.vector.tensor_copy(out=kw[:], in_=key_pool[:].indirect(slots[:]))
         nc.vector.tensor_copy(out=ks[:], in_=key_bytes[:].indirect(slots[:]))
-        nc.vector.tensor_scalar(out=neg_sharp[:], in0=sharp_col[:], scalar1=-1.0 / GROUP, scalar2=None, op0=ALU.mult)
 
         w_bf = [sb.tile([P, HALF, PACK], BF16, name=f"w_bf{h}", align_bytes=64) for h in range(2)]
         q_bf = sb.tile([P, Q, PACK], BF16, name="q_bf", align_bytes=64)
-        weave(nc.scalar.copy, q_bf[:], q_raw[:])
-        weave(nc.scalar.copy, w_bf[0][:], w_raw[0][:])
-        q_codes, q_scales = quantise("q", q_bf[:], Q)
-        score = psum.tile([P, I], F32, name="score", tag="acc")
-        nc.tensor.matmul_mx(out=score[:], lhsT=q_codes[:].bitcast(FP8X4), lhsT_scale=q_scales[:], rhs=kw[:].bitcast(FP4X4), rhs_scale=ks[:], start=True, stop=True)
-        w_q = [quantise("w0", w_bf[0][:], HALF)]
+        nc.scalar.copy(out=q_bf[:].rearrange("p (c i) t -> p c t i", i=4), in_=q_raw[:].rearrange("p t (c i) -> p c t i", i=4))
+        nc.gpsimd.tensor_scalar(out=neg_sharp[:], in0=sharp_col[:], scalar1=-1.0 / GROUP, scalar2=0.0, op0=ALU.mult, op1=ALU.add)
+        for h in range(2):
+            nc.gpsimd.tensor_scalar(out=w_bf[h][:], in0=w_raw[h][:].rearrange("p t c -> p c t"), scalar1=1.0, scalar2=0.0, op0=ALU.mult, op1=ALU.add)
+        q_codes, q_scales = quantise("q", q_bf[:].rearrange("p c t -> p (c t)"), Q)
+        score = []
+        for h in range(2):
+            bank = psum.tile([P, I // 2], F32, name=f"score{h}")
+            half = slice(h * I // 2, (h + 1) * I // 2)
+            nc.tensor.matmul_mx(out=bank[:], lhsT=q_codes[:].bitcast(FP8X4), lhsT_scale=q_scales[:], rhs=kw[:, half].bitcast(FP4X4), rhs_scale=ks[:, half], start=True, stop=True)
+            score.append(bank)
 
         p = sb.tile([P, I], F32, name="p")
+        pf = sb.tile([P, I], F32, name="pf")
         asum = sb.tile([P, G], F32, name="asum")
         nms = sb.tile([P, G], F32, name="nms")
         nmin = sb.tile([P, 1], F32, name="nmin")
@@ -117,56 +121,82 @@ def tile_attend_lrgated_bygroup_kernel(tc, query, keys_words, keys_scales, sharp
         rs = sb.tile([P, G], F32, name="rs")
         rz = sb.tile([P, 1], F32, name="rz")
         sh = sb.tile([P, G], F32, name="sh")
-        nc.vector.tensor_reduce(out=asum[:], in_=score[:].rearrange("q (g j) -> q g j", j=GROUP), axis=AX.X, op=ALU.add)
-        weave(nc.scalar.copy, w_bf[1][:], w_raw[1][:])
-        nc.scalar.activation(out=p[:], in_=score[:], func=ACT.Exp)
+        for h in range(2):
+            nc.vector.tensor_reduce(out=asum[:, h * G // 2 : (h + 1) * G // 2], in_=score[h][:].rearrange("q (g j) -> q g j", j=GROUP), axis=AX.X, op=ALU.add)
+            nc.scalar.activation(out=p[:, h * I // 2 : (h + 1) * I // 2], in_=score[h][:], func=ACT.Exp)
         nc.vector.tensor_scalar(out=nms[:], in0=asum[:], scalar1=neg_sharp[:], scalar2=None, op0=ALU.mult, op1=ALU.min, accum_out=nmin[:])
         nc.scalar.activation(out=pg[:], in_=nms[:], func=ACT.Exp, scale=-1.0, bias=nmin[:], accum_out=z[:])
-        nc.vector.tensor_copy(out=tw[:], in_=tab_wordt[:].indirect(slots[:]))
-        nc.vector.tensor_reduce(out=s[:], in_=p[:].rearrange("q (g j) -> q g j", j=GROUP), axis=AX.X, op=ALU.add)
+        nc.vector.tensor_copy(out=tw[:], in_=tab_pool[:].indirect(slots[:]))
         nc.vector.tensor_copy(out=ts[:], in_=tab_bytes[:].indirect(slots[:]))
-        nc.vector.reciprocal(out=rs[:], in_=s[:])
+        vf_rows = spread("vf_bank", vf_col, "score0")
+        wf_rows = spread("wf_bank", wf_col, "score1")
+        w_q = [quantise("w0", w_bf[0][:].rearrange("p c t -> p (c t)"), HALF)]
+        vf_row = sb.tile([P, I], F32, name="vf_row")
+        nc.vector.tensor_copy(out=vf_row[:].rearrange("p (n m) -> p n m", m=PACK), in_=vf_rows)
+        nc.vector.tensor_reduce(out=s[:], in_=p[:].rearrange("q (g j) -> q g j", j=GROUP), axis=AX.X, op=ALU.add)
         nc.vector.reciprocal(out=rz[:], in_=z[:])
-        w_q.append(quantise("w1", w_bf[1][:], HALF))
+        w_q.append(quantise("w1", w_bf[1][:].rearrange("p c t -> p (c t)"), HALF))
+        nc.vector.reciprocal(out=rs[:], in_=s[:])
+        nc.vector.tensor_tensor(out=pf[:].rearrange("p (n m) -> p n m", m=PACK), in0=wf_rows, in1=p[:].rearrange("p (n m) -> p n m", m=PACK), op=ALU.mult)
         nc.vector.scalar_tensor_tensor(out=sh[:], in0=pg[:], scalar=rz[:], in1=rs[:], op0=ALU.mult, op1=ALU.mult)
 
-        nc.vector.tensor_copy(out=cols[:], in_=cols_ps[:, 0, 0:8])
         zh = []
-        for j in range(4):
-            bank = zpsum.tile([P, I], F32, name=f"zh{j}")
+        for j in range(CHUNKS):
+            bank = psum.tile([P, I], F32, name=f"zh{j}", tag=f"bank{j}")
             codes, scales = w_q[j // 2]
             cs = slice(P * (j % 2), P * (j % 2 + 1))
             nc.tensor.matmul_mx(out=bank[:], lhsT=codes[:, cs].bitcast(FP8X4), lhsT_scale=scales[:, cs], rhs=tw[:].bitcast(FP4X4), rhs_scale=ts[:], start=True, stop=True)
             zh.append(bank)
 
         def dealt(ap):
-            return ap.rearrange("p (b t j) -> p t b j", t=PACK, j=GROUP)
+            return ap.rearrange("p (b u x) -> p b u x", u=2, x=16)
 
-        def turn_scale_quantise(name, src, factor):
-            turned = psum.tile([P, PACK, P], F32, name=name + "_turned", tag="turn")
-            for t in range(PACK):
-                nc.tensor.transpose(turned[:, t, :], src[:, t, :], ident[:])
-            woven = ring.tile([P, P, PACK], BF16, name=name + "_woven", tag="woven", align_bytes=64)
-            nc.vector.tensor_tensor(out=woven[:], in0=turned[:].rearrange("p t c -> p c t"), in1=factor.unsqueeze(1).to_broadcast([P, P, PACK]), op=ALU.mult)
-            return quantise(name, woven[:], P)
+        def place(tile):
+            return tile[:].rearrange("p u (b x) -> p b u x", x=16)
 
-        w = ring.tile([P, PACK, P], F32, name="w", tag="dealt")
+        def turn(name, pairs, tag):
+            turned = psum.tile([P, 2, P], F32, name=name, tag=tag)
+            for u in range(2):
+                nc.tensor.transpose(turned[:, u, :], pairs[:, u, :].bitcast(F32), ident[:])
+            return turned
+
+        w = sb.tile([P, 2, I // 2], BF16, name="w")
         nc.vector.tensor_tensor(
-            out=w[:].rearrange("p t (b j) -> p t b j", j=GROUP), in0=dealt(p[:]),
-            in1=sh[:].rearrange("p (b t) -> p t b", t=PACK).unsqueeze(3).to_broadcast([P, PACK, P // GROUP, GROUP]), op=ALU.mult)
-        wt_codes, wt_scales = turn_scale_quantise("wt", w, cols[:, 4:8])
+            out=w[:].rearrange("p u (b h j) -> p b u h j", h=2, j=GROUP),
+            in0=pf[:].rearrange("p (b u h j) -> p b u h j", u=2, h=2, j=GROUP),
+            in1=sh[:].rearrange("p (b u h) -> p b u h", u=2, h=2).unsqueeze(4).to_broadcast([P, 16, 2, 2, GROUP]), op=ALU.mult)
+        w_turned = turn("wt", w, "wt")
 
-        for j in range(4):
-            hg = ring.tile([P, I], F32, name=f"hg{j}", tag="hg", bufs=4)
+        last = CHUNKS - 1
+        zv = sb.tile([P, I], F32, name="zv")
+        nc.vector.tensor_tensor(out=zv[:], in0=zh[last][:], in1=vf_row[:], op=ALU.mult)
+        turned = []
+        for j in range(CHUNKS):
+            hg = sb.tile([P, I], F32, name=f"hg{j}")
             nc.scalar.activation(out=hg[:], in_=g_raw[j][:].indirect(gates[:]), func=ACT.Sigmoid)
-            hv = ring.tile([P, PACK, P], F32, name=f"hv{j}", tag="dealt")
-            nc.vector.tensor_tensor(out=hv[:].rearrange("p t (b j) -> p t b j", j=GROUP), in0=dealt(zh[j][:]), in1=dealt(hg[:]), op=ALU.mult)
-            h_codes, h_scales = turn_scale_quantise(f"ht{j}", hv, cols[:, 0:4])
-            if j in (0, 3):
-                acc = psum.tile([P, I], F32, name=f"acc{j}", tag="acc")
+            hw = sb.tile([P, 2, I // 2], BF16, name=f"hw{j}")
+            if j < last:
+                gv = sb.tile([P, I], F32, name=f"gv{j}")
+                nc.gpsimd.tensor_tensor(out=gv[:], in0=hg[:], in1=vf_row[:], op=ALU.mult)
+                nc.vector.tensor_tensor(out=place(hw), in0=dealt(zh[j][:]), in1=dealt(gv[:]), op=ALU.mult)
+            else:
+                nc.vector.tensor_tensor(out=place(hw), in0=dealt(zv[:]), in1=dealt(hg[:]), op=ALU.mult)
+            turned.append(turn(f"ht{j}", hw, f"bank{j}"))
+
+        woven = sb.tile([P, CHUNKS + 1, P, 2], F32, name="woven", tag="g_raw3", align_bytes=64)
+
+        def weave_quantise(name, n, src):
+            nc.scalar.copy(out=woven[:, n], in_=src[:].rearrange("p u c -> p c u"))
+            return quantise(name, woven[:, n].rearrange("p c u -> p (c u)").bitcast(BF16), P)
+
+        wt_codes, wt_scales = weave_quantise("wt", CHUNKS, w_turned)
+        for j in range(CHUNKS):
+            h_codes, h_scales = weave_quantise(f"ht{j}", j, turned[j])
+            if j in (0, CHUNKS - 1):
+                acc = psum.tile([P, R], F32, name=f"acc{j}", tag="acc" if j == 0 else "score0")
             nc.tensor.matmul_mx(out=acc[:, P * j : P * (j + 1)], lhsT=wt_codes[:].bitcast(FP8X4), lhsT_scale=wt_scales[:], rhs=h_codes[:].bitcast(FP8X4), rhs_scale=h_scales[:], start=True, stop=True)
-            if j >= 2:
-                rs_ = slice(0, 3 * P) if j == 2 else slice(3 * P, R)
+            if j >= CHUNKS - 2:
+                cols = slice(0, 3 * P) if j == CHUNKS - 2 else slice(3 * P, R)
                 res = sb.tile([P, R], F32, name=f"res{j}")
-                nc.scalar.copy(out=res[:, rs_], in_=acc[:, rs_])
-                nc.sync.dma_start(out=out[:, rs_], in_=res[:, rs_])
+                nc.vector.tensor_copy(out=res[:, cols], in_=acc[:, cols]) if j == CHUNKS - 2 else nc.scalar.copy(out=res[:, cols], in_=acc[:, cols])
+                nc.sync.dma_start(out=out[:, cols], in_=res[:, cols])

from contextlib import ExitStack

import concourse.mybir as mybir
from concourse.masks import make_identity

D, K, R, T, I, Q, G, U = 512, 512, 512, 2048, 512, 128, 64, 1024
FLOPS = 2 * (D * Q * I + K * R * I + I * Q * R)

F32 = mybir.dt.float32
BF16 = mybir.dt.bfloat16
I32 = mybir.dt.int32
U32 = mybir.dt.uint32
U16 = mybir.dt.uint16
U8 = mybir.dt.uint8
FP8X4 = mybir.dt.float8_e4m3fn_x4
FP4X4 = mybir.dt.float4_e2m1fn_x4
ALU = mybir.AluOpType
ACT = mybir.ActivationFunctionType
AX = mybir.AxisListType

P = 128
PACK = 4
GROUP = I // G
HALF = R // 2
CHUNKS = R // P


def tile_attend_lrgated_bygroup_kernel(tc, query, keys_words, keys_scales, sharp, tab_words, tab_scales, w1, gtab, w_factor, v_factor, offs2, offs, out):
    nc = tc.nc
    with ExitStack() as ctx:
        lists = ctx.enter_context(tc.tile_pool(name="lists", bufs=1))
        sb = ctx.enter_context(tc.tile_pool(name="sb", bufs=1))
        psum = ctx.enter_context(tc.psum_pool(name="psum", bufs=1))

        slots = lists.tile([P, I // 16], U16, name="slots")
        gates = lists.tile([P, I // 16], U16, name="gates")
        key_pool = sb.tile([P, T], U16, name="key_pool")
        tab_pool = sb.tile([P, T], U16, name="tab_pool")
        key_bytes = sb.tile([P, T], U8, name="key_bytes")
        tab_bytes = sb.tile([P, T], U8, name="tab_bytes")
        q_raw = sb.tile([P, PACK, Q], F32, name="q_raw")
        w_raw = [sb.tile([P, PACK, HALF], F32, name=f"w_raw{h}") for h in range(2)]
        g_raw = [sb.tile([P, U], F32, name=f"g_raw{j}", align_bytes=64) for j in range(CHUNKS)]
        ident = sb.tile([P, P], F32, name="ident")
        warm = sb.tile([P, 1], F32, name="warm")
        warm2 = sb.tile([P, 1], F32, name="warm2")
        sharp_col = sb.tile([P, 1], F32, name="sharp_col")
        wf_col = sb.tile([P, PACK], F32, name="wf_col")
        vf_col = sb.tile([P, PACK], F32, name="vf_col")

        nc.gpsimd.memset(key_bytes[:].bitcast(I32), 0)
        nc.vector.memset(warm[:], 0.0)
        nc.vector.memset(tab_bytes[:].bitcast(I32), 0)
        nc.scalar.activation(out=warm2[:], in_=warm[:], func=ACT.Exp)
        nc.gpsimd.dma_start(out=sharp_col[:], in_=sharp)
        nc.gpsimd.dma_start(out=vf_col[:], in_=v_factor.rearrange("o (n m) -> (o n) m", m=PACK))
        make_identity(nc, ident[:])
        nc.gpsimd.dma_start(out=wf_col[:], in_=w_factor.rearrange("o (n m) -> (o n) m", m=PACK))

        def load_scales(tile, src):
            for quad in range(4):
                nc.sync.dma_start(out=tile[32 * quad : 32 * quad + 4, :].bitcast(I32), in_=src[0, 4 * quad : 4 * quad + 4, :].bitcast(I32))

        w_view = w1.rearrange("(p t) r -> p t r", t=PACK)
        nc.sync.dma_start(slots[:], offs)
        nc.sync.dma_start(out=key_pool[:].bitcast(I32), in_=keys_words[0].bitcast(I32))
        load_scales(key_bytes, keys_scales)
        nc.sync.dma_start(out=q_raw[:], in_=query.rearrange("(p t) q -> p t q", t=PACK))
        nc.sync.dma_start(out=tab_pool[:].bitcast(I32), in_=tab_words[0].bitcast(I32))
        nc.sync.dma_start(out=w_raw[0][:], in_=w_view[:, :, 0:HALF])
        load_scales(tab_bytes, tab_scales)
        nc.sync.dma_start(gates[:], offs2)
        nc.sync.dma_start(out=g_raw[0][:], in_=gtab[0:P, :])
        nc.sync.dma_start(out=w_raw[1][:], in_=w_view[:, :, HALF:R])
        for j in range(1, CHUNKS):
            nc.sync.dma_start(out=g_raw[j][:], in_=gtab[P * j : P * (j + 1), :])

        def spread(name, col, tag):
            bank = psum.tile([P, PACK, P], F32, name=name, tag=tag)
            for m in range(PACK):
                nc.tensor.transpose(bank[:, m, :], col[:, m : m + 1].to_broadcast([P, P]), ident[:])
            return bank[:].rearrange("p m n -> p n m")

        def quantise(name, src, width):
            codes = sb.tile([P, width], U32, name=name + "_codes", align_bytes=64)
            scales = sb.tile([P, width], U8, name=name + "_scales", align_bytes=64)
            nc.vector.quantize_mx(out=codes[:].bitcast(FP8X4), scales=scales[:], in_=src)
            return codes, scales


        kw = sb.tile([P, I], U16, name="kw", align_bytes=64)
        ks = sb.tile([P, I], U8, name="ks", align_bytes=64)
        tw = sb.tile([P, I], U16, name="tw", align_bytes=64)
        ts = sb.tile([P, I], U8, name="ts", align_bytes=64)
        neg_sharp = sb.tile([P, 1], F32, name="neg_sharp")
        nc.vector.tensor_copy(out=kw[:], in_=key_pool[:].indirect(slots[:]))
        nc.vector.tensor_copy(out=ks[:], in_=key_bytes[:].indirect(slots[:]))

        w_bf = [sb.tile([P, HALF, PACK], BF16, name=f"w_bf{h}", align_bytes=64) for h in range(2)]
        q_bf = sb.tile([P, Q, PACK], BF16, name="q_bf", align_bytes=64)
        nc.scalar.copy(out=q_bf[:].rearrange("p (c i) t -> p c t i", i=4), in_=q_raw[:].rearrange("p t (c i) -> p c t i", i=4))
        nc.gpsimd.tensor_scalar(out=neg_sharp[:], in0=sharp_col[:], scalar1=-1.0 / GROUP, scalar2=0.0, op0=ALU.mult, op1=ALU.add)
        for h in range(2):
            nc.gpsimd.tensor_scalar(out=w_bf[h][:], in0=w_raw[h][:].rearrange("p t c -> p c t"), scalar1=1.0, scalar2=0.0, op0=ALU.mult, op1=ALU.add)
        q_codes, q_scales = quantise("q", q_bf[:].rearrange("p c t -> p (c t)"), Q)
        score = []
        for h in range(2):
            bank = psum.tile([P, I // 2], F32, name=f"score{h}")
            half = slice(h * I // 2, (h + 1) * I // 2)
            nc.tensor.matmul_mx(out=bank[:], lhsT=q_codes[:].bitcast(FP8X4), lhsT_scale=q_scales[:], rhs=kw[:, half].bitcast(FP4X4), rhs_scale=ks[:, half], start=True, stop=True)
            score.append(bank)

        p = sb.tile([P, I], F32, name="p")
        pf = sb.tile([P, I], F32, name="pf")
        asum = sb.tile([P, G], F32, name="asum")
        nms = sb.tile([P, G], F32, name="nms")
        nmin = sb.tile([P, 1], F32, name="nmin")
        pg = sb.tile([P, G], F32, name="pg")
        z = sb.tile([P, 1], F32, name="z")
        s = sb.tile([P, G], F32, name="s")
        rs = sb.tile([P, G], F32, name="rs")
        rz = sb.tile([P, 1], F32, name="rz")
        sh = sb.tile([P, G], F32, name="sh")
        for h in range(2):
            nc.vector.tensor_reduce(out=asum[:, h * G // 2 : (h + 1) * G // 2], in_=score[h][:].rearrange("q (g j) -> q g j", j=GROUP), axis=AX.X, op=ALU.add)
            nc.scalar.activation(out=p[:, h * I // 2 : (h + 1) * I // 2], in_=score[h][:], func=ACT.Exp)
        nc.vector.tensor_scalar(out=nms[:], in0=asum[:], scalar1=neg_sharp[:], scalar2=None, op0=ALU.mult, op1=ALU.min, accum_out=nmin[:])
        nc.scalar.activation(out=pg[:], in_=nms[:], func=ACT.Exp, scale=-1.0, bias=nmin[:], accum_out=z[:])
        nc.vector.tensor_copy(out=tw[:], in_=tab_pool[:].indirect(slots[:]))
        nc.vector.tensor_copy(out=ts[:], in_=tab_bytes[:].indirect(slots[:]))
        vf_rows = spread("vf_bank", vf_col, "score0")
        wf_rows = spread("wf_bank", wf_col, "score1")
        w_q = [quantise("w0", w_bf[0][:].rearrange("p c t -> p (c t)"), HALF)]
        vf_row = sb.tile([P, I], F32, name="vf_row")
        nc.vector.tensor_copy(out=vf_row[:].rearrange("p (n m) -> p n m", m=PACK), in_=vf_rows)
        nc.vector.tensor_reduce(out=s[:], in_=p[:].rearrange("q (g j) -> q g j", j=GROUP), axis=AX.X, op=ALU.add)
        nc.vector.reciprocal(out=rz[:], in_=z[:])
        w_q.append(quantise("w1", w_bf[1][:].rearrange("p c t -> p (c t)"), HALF))
        nc.vector.reciprocal(out=rs[:], in_=s[:])
        nc.vector.tensor_tensor(out=pf[:].rearrange("p (n m) -> p n m", m=PACK), in0=wf_rows, in1=p[:].rearrange("p (n m) -> p n m", m=PACK), op=ALU.mult)
        nc.vector.scalar_tensor_tensor(out=sh[:], in0=pg[:], scalar=rz[:], in1=rs[:], op0=ALU.mult, op1=ALU.mult)

        zh = []
        for j in range(CHUNKS):
            bank = psum.tile([P, I], F32, name=f"zh{j}", tag=f"bank{j}")
            codes, scales = w_q[j // 2]
            cs = slice(P * (j % 2), P * (j % 2 + 1))
            nc.tensor.matmul_mx(out=bank[:], lhsT=codes[:, cs].bitcast(FP8X4), lhsT_scale=scales[:, cs], rhs=tw[:].bitcast(FP4X4), rhs_scale=ts[:], start=True, stop=True)
            zh.append(bank)

        def dealt(ap):
            return ap.rearrange("p (b u x) -> p b u x", u=2, x=16)

        def place(tile):
            return tile[:].rearrange("p u (b x) -> p b u x", x=16)

        def turn(name, pairs, tag):
            turned = psum.tile([P, 2, P], F32, name=name, tag=tag)
            for u in range(2):
                nc.tensor.transpose(turned[:, u, :], pairs[:, u, :].bitcast(F32), ident[:])
            return turned

        w = sb.tile([P, 2, I // 2], BF16, name="w")
        nc.vector.tensor_tensor(
            out=w[:].rearrange("p u (b h j) -> p b u h j", h=2, j=GROUP),
            in0=pf[:].rearrange("p (b u h j) -> p b u h j", u=2, h=2, j=GROUP),
            in1=sh[:].rearrange("p (b u h) -> p b u h", u=2, h=2).unsqueeze(4).to_broadcast([P, 16, 2, 2, GROUP]), op=ALU.mult)
        w_turned = turn("wt", w, "wt")

        last = CHUNKS - 1
        zv = sb.tile([P, I], F32, name="zv")
        nc.vector.tensor_tensor(out=zv[:], in0=zh[last][:], in1=vf_row[:], op=ALU.mult)
        turned = []
        for j in range(CHUNKS):
            hg = sb.tile([P, I], F32, name=f"hg{j}")
            nc.scalar.activation(out=hg[:], in_=g_raw[j][:].indirect(gates[:]), func=ACT.Sigmoid)
            hw = sb.tile([P, 2, I // 2], BF16, name=f"hw{j}")
            if j < last:
                gv = sb.tile([P, I], F32, name=f"gv{j}")
                nc.gpsimd.tensor_tensor(out=gv[:], in0=hg[:], in1=vf_row[:], op=ALU.mult)
                nc.vector.tensor_tensor(out=place(hw), in0=dealt(zh[j][:]), in1=dealt(gv[:]), op=ALU.mult)
            else:
                nc.vector.tensor_tensor(out=place(hw), in0=dealt(zv[:]), in1=dealt(hg[:]), op=ALU.mult)
            turned.append(turn(f"ht{j}", hw, f"bank{j}"))

        woven = sb.tile([P, CHUNKS + 1, P, 2], F32, name="woven", tag="g_raw3", align_bytes=64)

        def weave_quantise(name, n, src):
            nc.scalar.copy(out=woven[:, n], in_=src[:].rearrange("p u c -> p c u"))
            return quantise(name, woven[:, n].rearrange("p c u -> p (c u)").bitcast(BF16), P)

        wt_codes, wt_scales = weave_quantise("wt", CHUNKS, w_turned)
        for j in range(CHUNKS):
            h_codes, h_scales = weave_quantise(f"ht{j}", j, turned[j])
            if j in (0, CHUNKS - 1):
                acc = psum.tile([P, R], F32, name=f"acc{j}", tag="acc" if j == 0 else "score0")
            nc.tensor.matmul_mx(out=acc[:, P * j : P * (j + 1)], lhsT=wt_codes[:].bitcast(FP8X4), lhsT_scale=wt_scales[:], rhs=h_codes[:].bitcast(FP8X4), rhs_scale=h_scales[:], start=True, stop=True)
            if j >= CHUNKS - 2:
                cols = slice(0, 3 * P) if j == CHUNKS - 2 else slice(3 * P, R)
                res = sb.tile([P, R], F32, name=f"res{j}")
                nc.vector.tensor_copy(out=res[:, cols], in_=acc[:, cols]) if j == CHUNKS - 2 else nc.scalar.copy(out=res[:, cols], in_=acc[:, cols])
                nc.sync.dma_start(out=out[:, cols], in_=res[:, cols])
